import numpy as np
import ml_dtypes


def mxq(x, axis, fmt="e4m3"):
    dtype, down = {"e4m3": (ml_dtypes.float8_e4m3fn, 7), "e5m2": (ml_dtypes.float8_e5m2, 14)}[fmt]
    v = np.moveaxis(np.asarray(x, np.float32).astype(ml_dtypes.bfloat16).astype(np.float64), axis, -1)
    blocks = v.reshape(v.shape[:-1] + (-1, 32))
    amax = np.abs(blocks).max(-1, keepdims=True)
    byte = np.maximum(np.where(amax > 0, np.frexp(amax)[1] - 1 + 127, 0) - down, 1)
    scale = np.exp2(byte - 127.0)
    codes = (blocks / scale).astype(np.float32).astype(dtype).astype(np.float64)
    return np.moveaxis((codes * scale).reshape(v.shape), -1, axis)


WIDE = False


def mx_kscale(k):
    if not WIDE:
        return np.ones(k)
    levels = np.array([10, -10, 5, -5, 0])
    if k % 512:
        return np.exp2(np.random.permutation(np.resize(levels, k // 32))).repeat(32)
    a = np.empty((k // 512, 16))
    for p in range(k // 512):
        a[p, :8] = np.random.permutation(np.resize(levels, 8))
        for g in range(8):
            far = levels[np.abs(levels - a[p, g]) >= 10]
            a[p, g + 8] = far[np.random.randint(len(far))]
    return np.exp2(a.ravel()).repeat(32)


def f64(x):
    return np.asarray(x).astype(np.float64)


def striped(idx):
    return np.tile(idx.reshape(-1, 16).T, (8, 1)).astype(np.uint16)


def unstriped(offs):
    return offs[:16].T.reshape(-1).astype(np.int64)


def silu(v):
    return v / (1.0 + np.exp(-np.maximum(v, -700.0)))


K, T, E, C, H, N = 512, 1024, 8, 128, 512, 256


def by_expert(wq, xq):
    return np.concatenate([wq[e].T @ xq[:, e * C:(e + 1) * C] for e in range(E)], axis=1)


def setup_inputs():
    n = np.random.standard_normal
    s = mx_kscale(K)[:, None]
    u = mx_kscale(H)
    return {
        "xT": (n((K, T)) * s).astype(np.float32),
        "w1": (n((E, K, H)) / np.sqrt(K) / s[None] * u[None, None, :]).astype(np.float32),
        "w2": (n((E, H, N)) / np.sqrt(H) / u[None, :, None]).astype(np.float32),
        "gate": np.tile(np.random.uniform(0.2, 1.0, E * C), (N, 1)).astype(np.float32),
        "offs": striped(np.random.permutation(T)[:E * C]),
    }


def reference(xT, w1, w2, gate, offs):
    idx = unstriped(offs)
    xq = mxq(f64(xT)[:, idx], 0, "e4m3")
    h = silu(by_expert(mxq(f64(w1), 1, "e4m3"), xq))
    y = by_expert(mxq(f64(w2), 1, "e4m3"), mxq(h, 0, "e4m3"))
    out = np.zeros((N, T))
    out[:, idx] = f64(gate) * y
    return out

@@ -1,0 +1,229 @@
+from contextlib import ExitStack
+
+import concourse.mybir as mybir
+
+K, T, E, C, H, N = 512, 1024, 8, 128, 512, 256
+FLOPS = 2 * E * C * (K * H + H * N)
+
+F32 = mybir.dt.float32
+BF16 = mybir.dt.bfloat16
+U32 = mybir.dt.uint32
+U16 = mybir.dt.uint16
+U8 = mybir.dt.uint8
+FP8X4 = mybir.dt.float8_e4m3fn_x4
+SILU = mybir.ActivationFunctionType.Silu
+MULT = mybir.AluOpType.mult
+ADD = mybir.AluOpType.add
+
+P = 128
+HALF = 512
+LOAD_ORDER = (
+    (1, 0), (2, 0), (1, 1), (2, 1), (0, 0), (1, 2), (2, 2), (1, 3), (2, 3), (1, 4), (2, 4),
+    (1, 5), (1, 6), (1, 7), (0, 1), (2, 5), (2, 6), (2, 7),
+)
+V_TOK = (320, 0)
+
+
+def tile_routed_moe_kernel(tc, xT, w1, w2, gate, offs, out):
+    nc = tc.nc
+    with ExitStack() as ctx:
+        keep = ctx.enter_context(tc.tile_pool(name="keep", bufs=1))
+        stage = ctx.enter_context(tc.tile_pool(name="stage", bufs=3))
+        single = ctx.enter_context(tc.tile_pool(name="single", bufs=2))
+        hbank = ctx.enter_context(tc.psum_pool(name="hbank", bufs=3))
+        ybank = ctx.enter_context(tc.psum_pool(name="ybank", bufs=3))
+
+        offs_sb = keep.tile([P, E * C // 16], U16, name="offs_sb")
+        nc.sync.dma_start(offs_sb[:], offs)
+        x_view = xT.rearrange("(p t) n -> p t n", t=4)
+        x_raw = []
+        for u in range(2):
+            for v in range(2):
+                xr = keep.tile([P, 2, HALF], F32, name="x_raw%d%d" % (u, v))
+                nc.sync.dma_start(xr[:], x_view[:, 2 * u : 2 * u + 2, v * HALF : (v + 1) * HALF])
+                x_raw.append(xr)
+        w1_raw = []
+        w2_raw = []
+        gate_sb = []
+        gate_view = gate.rearrange("(b p) s -> p b s", p=P)
+        for e in range(E):
+            r1 = keep.tile([P, 4, H], F32, name="w1_raw%d" % e)
+            w1_raw.append(r1)
+            r2 = keep.tile([P, 4, N], F32, name="w2_raw%d" % e)
+            w2_raw.append(r2)
+        for v in range(2):
+            gt = keep.tile([P, 2, HALF], F32, name="gate_sb%d" % v)
+            gate_sb.append(gt)
+        for kind, i in LOAD_ORDER:
+            if kind == 1:
+                nc.sync.dma_start(w1_raw[i][:], w1[i].rearrange("(p j) c -> p j c", j=4))
+            elif kind == 2:
+                nc.sync.dma_start(w2_raw[i][:], w2[i].rearrange("(p j) c -> p j c", j=4))
+            else:
+                nc.sync.dma_start(gate_sb[i][:], gate_view[:, :, i * HALF : (i + 1) * HALF])
+
+        warm_in = keep.tile([P, 1], F32, name="warm_in")
+        warm_out = keep.tile([P, 1], F32, name="warm_out")
+        nc.vector.memset(warm_in[:], 0.0)
+        nc.scalar.activation(out=warm_out[:], in_=warm_in[:], func=SILU)
+
+        x_pair = []
+        for u in range(2):
+            xb = keep.tile([P, T, 2], BF16, name="x_pair%d" % u)
+            x_pair.append(xb)
+            for v in range(2):
+                src = x_raw[2 * u + v][:].rearrange("p e (c i) -> p c e i", i=4)
+                dst = xb[:, v * HALF : (v + 1) * HALF, :].rearrange("p (c i) e -> p c e i", i=4)
+                cut = V_TOK[u] // 4
+                if cut > 0:
+                    nc.vector.tensor_copy(out=dst[:, :cut], in_=src[:, :cut])
+                nc.scalar.copy(out=dst[:, cut:], in_=src[:, cut:])
+        x_grp = []
+        for g in range(2):
+            xg = keep.tile([P, HALF, 4], BF16, name="x_grp%d" % g, align_bytes=64)
+            x_grp.append(xg)
+        x_codes = []
+        x_scales = []
+
+        def gather(u, g):
+            window = x_pair[u][:].rearrange("p n e -> p (n e)").bitcast(U32)
+            words = x_grp[g][:].rearrange("p s j -> p (s j)").bitcast(U32).rearrange("p (s u) -> p s u", u=2)
+            cols = HALF // 16
+            nc.vector.tensor_copy(out=words[:, :, u], in_=window.indirect(offs_sb[:, g * cols : (g + 1) * cols]))
+
+        def quantise_x(g):
+            xc = keep.tile([P, HALF], U32, name="x_codes%d" % g, align_bytes=64)
+            xs = keep.tile([P, HALF], U8, name="x_scales%d" % g, align_bytes=64)
+            nc.vector.quantize_mx(out=xc[:].bitcast(FP8X4), scales=xs[:], in_=x_grp[g][:].rearrange("p s j -> p (s j)"))
+            x_codes.append(xc)
+            x_scales.append(xs)
+
+        gather(0, 0)
+        gather(0, 1)
+
+        win = []
+        for b in range(2):
+            wt = keep.tile([P, T], F32, name="win%d" % b)
+            win.append(wt)
+
+        live = {}
+
+        def copy_w1(e):
+            g1 = stage.tile([P, 4 * H], BF16, name="g1", align_bytes=64)
+            nc.scalar.copy(
+                out=g1[:].rearrange("p (t m j) -> p m j t", t=4, j=4),
+                in_=w1_raw[e][:].rearrange("p j (m t) -> p m j t", t=4),
+            )
+            live[("g1", e)] = g1
+
+        def quantise_w1(e):
+            c1 = stage.tile([P, H], U32, name="c1", align_bytes=64)
+            s1 = stage.tile([P, H], U8, name="s1", align_bytes=64)
+            nc.vector.quantize_mx(out=c1[:].bitcast(FP8X4), scales=s1[:], in_=live[("g1", e)][:])
+            live[("c1", e)] = c1
+            live[("s1", e)] = s1
+
+        def copy_w2(e):
+            g2 = single.tile([P, N, 4], BF16, name="g2", align_bytes=64)
+            nc.gpsimd.tensor_scalar(
+                out=g2[:], in0=w2_raw[e][:].rearrange("p j c -> p c j"), scalar1=1.0, scalar2=0.0, op0=MULT, op1=ADD
+            )
+            live[("g2", e)] = g2
+
+        def quantise_w2(e):
+            c2 = stage.tile([P, N], U32, name="c2", align_bytes=64)
+            s2 = stage.tile([P, N], U8, name="s2", align_bytes=64)
+            nc.vector.quantize_mx(out=c2[:].bitcast(FP8X4), scales=s2[:], in_=live[("g2", e)][:].rearrange("p c j -> p (c j)"))
+            live[("c2", e)] = c2
+            live[("s2", e)] = s2
+
+        def layer1(e):
+            g = e * C // HALF
+            s0 = e * C - g * HALF
+            ph = hbank.tile([P, 4, C], F32, name="ph")
+            for t in range(4):
+                nc.tensor.matmul_mx(
+                    out=ph[:, t, :],
+                    lhsT=live[("c1", e)][:, t * P : (t + 1) * P].bitcast(FP8X4),
+                    lhsT_scale=live[("s1", e)][:, t * P : (t + 1) * P],
+                    rhs=x_codes[g][:, s0 : s0 + C].bitcast(FP8X4),
+                    rhs_scale=x_scales[g][:, s0 : s0 + C],
+                    start=True,
+                    stop=True,
+                )
+            live[("ph", e)] = ph
+
+        def silu(e):
+            hg = stage.tile([P, C, 4], BF16, name="hg", align_bytes=64)
+            nc.scalar.activation(out=hg[:], in_=live[("ph", e)][:].rearrange("p t s -> p s t"), func=SILU)
+            live[("hg", e)] = hg
+
+        def quantise_h(e):
+            hc = stage.tile([P, C], U32, name="hc", align_bytes=64)
+            hs = stage.tile([P, C], U8, name="hs", align_bytes=64)
+            nc.vector.quantize_mx(out=hc[:].bitcast(FP8X4), scales=hs[:], in_=live[("hg", e)][:].rearrange("p s t -> p (s t)"))
+            live[("hc", e)] = hc
+            live[("hs", e)] = hs
+
+        def layer2(e):
+            py = ybank.tile([P, 2, C], F32, name="py")
+            for b in range(2):
+                nc.tensor.matmul_mx(
+                    out=py[:, b, :],
+                    lhsT=live[("c2", e)][:, b * P : (b + 1) * P].bitcast(FP8X4),
+                    lhsT_scale=live[("s2", e)][:, b * P : (b + 1) * P],
+                    rhs=live[("hc", e)][:].bitcast(FP8X4),
+                    rhs_scale=live[("hs", e)][:],
+                    start=True,
+                    stop=True,
+                )
+            live[("py", e)] = py
+
+        def empty_y(e):
+            g = e * C // HALF
+            s0 = e * C - g * HALF
+            ys = stage.tile([P, 2, C], F32, name="ys")
+            nc.scalar.copy(out=ys[:], in_=live[("py", e)][:])
+            live[("ys", e)] = ys
+
+        def scatter(e, b):
+            g = e * C // HALF
+            s0 = e * C - g * HALF
+            nc.vector.tensor_tensor(
+                out=win[b][:].indirect(offs_sb[:, e * (C // 16) : (e + 1) * (C // 16)]),
+                in0=live[("ys", e)][:, b, :],
+                in1=gate_sb[g][:, b, s0 : s0 + C],
+                op=MULT,
+            )
+
+        copy_w2(0)
+        gather(1, 0)
+        quantise_x(0)
+        for p in range(-2, E):
+            if 1 <= p + 3 < E:
+                copy_w2(p + 3)
+            if p + 2 < E:
+                copy_w1(p + 2)
+            if 0 <= p + 1 < E:
+                silu(p + 1)
+            if p + 2 < E:
+                quantise_w1(p + 2)
+                layer1(p + 2)
+            if p == -2:
+                quantise_w2(0)
+            if 0 <= p + 1 < E:
+                quantise_h(p + 1)
+                layer2(p + 1)
+            if 1 <= p + 3 < E:
+                quantise_w2(p + 3)
+            if p == -2:
+                gather(1, 1)
+                quantise_x(1)
+            if 0 <= p:
+                scatter(p, 1)
+            if 0 <= p + 1 < E:
+                empty_y(p + 1)
+                scatter(p + 1, 0)
+
+        for b in range(2):
+            nc.sync.dma_start(out[b * P : (b + 1) * P, :], win[b][:])

@@ -16,6 +16,7 @@ MULT = mybir.AluOpType.mult
 ADD = mybir.AluOpType.add
 
 P = 128
+W1_BYTES = 4 * H * 4
 HALF = 512
 LOAD_ORDER = (
     (1, 0), (2, 0), (1, 1), (2, 1), (0, 0), (1, 2), (2, 2), (1, 3), (2, 3), (1, 4), (2, 4),
@@ -30,6 +31,7 @@ def tile_routed_moe_kernel(tc, xT, w1, w2, gate, offs, out):
         keep = ctx.enter_context(tc.tile_pool(name="keep", bufs=1))
         stage = ctx.enter_context(tc.tile_pool(name="stage", bufs=3))
         single = ctx.enter_context(tc.tile_pool(name="single", bufs=2))
+        raw1 = ctx.enter_context(tc.tile_pool(name="raw1", bufs=1))
         hbank = ctx.enter_context(tc.psum_pool(name="hbank", bufs=3))
         ybank = ctx.enter_context(tc.psum_pool(name="ybank", bufs=3))
 
@@ -47,7 +49,7 @@ def tile_routed_moe_kernel(tc, xT, w1, w2, gate, offs, out):
         gate_sb = []
         gate_view = gate.rearrange("(b p) s -> p b s", p=P)
         for e in range(E):
-            r1 = keep.tile([P, 4, H], F32, name="w1_raw%d" % e)
+            r1 = raw1.tile([P, 4, H], F32, name="w1_raw%d" % e, offset=e * W1_BYTES, align_bytes=64)
             w1_raw.append(r1)
             r2 = keep.tile([P, 4, N], F32, name="w2_raw%d" % e)
             w2_raw.append(r2)
@@ -154,7 +156,9 @@ def tile_routed_moe_kernel(tc, xT, w1, w2, gate, offs, out):
             live[("ph", e)] = ph
 
         def silu(e):
-            hg = stage.tile([P, C, 4], BF16, name="hg", align_bytes=64)
+            hg = raw1.tile(
+                [P, C, 4], BF16, name="hg%d" % e, offset=min(e + 1, E - 1) * W1_BYTES + (e + 1) // E * 2048, align_bytes=64
+            )
             nc.scalar.activation(out=hg[:], in_=live[("ph", e)][:].rearrange("p t s -> p s t"), func=SILU)
             live[("hg", e)] = hg
 
@@ -182,7 +186,9 @@ def tile_routed_moe_kernel(tc, xT, w1, w2, gate, offs, out):
         def empty_y(e):
             g = e * C // HALF
             s0 = e * C - g * HALF
-            ys = stage.tile([P, 2, C], F32, name="ys")
+            ys = raw1.tile(
+                [P, 2, C], F32, name="ys%d" % e, offset=min(e + 2, E - 1) * W1_BYTES + 1024 + max(e + 3 - E, 0) * 2048, align_bytes=64
+            )
             nc.scalar.copy(out=ys[:], in_=live[("py", e)][:])
             live[("ys", e)] = ys
 
@@ -206,6 +212,8 @@ def tile_routed_moe_kernel(tc, xT, w1, w2, gate, offs, out):
                 copy_w1(p + 2)
             if 0 <= p + 1 < E:
                 silu(p + 1)
+            if 0 <= p:
+                empty_y(p)
             if p + 2 < E:
                 quantise_w1(p + 2)
                 layer1(p + 2)
@@ -220,10 +228,8 @@ def tile_routed_moe_kernel(tc, xT, w1, w2, gate, offs, out):
                 gather(1, 1)
                 quantise_x(1)
             if 0 <= p:
+                scatter(p, 0)
                 scatter(p, 1)
-            if 0 <= p + 1 < E:
-                empty_y(p + 1)
-                scatter(p + 1, 0)
 
         for b in range(2):
             nc.sync.dma_start(out[b * P : (b + 1) * P, :], win[b][:])

@@ -127,8 +127,9 @@ def tile_routed_moe_kernel(tc, xT, w1, w2, gate, offs, out):
 
         def copy_w2(e):
             g2 = single.tile([P, N, 4], BF16, name="g2", align_bytes=64)
-            nc.gpsimd.tensor_scalar(
-                out=g2[:], in0=w2_raw[e][:].rearrange("p j c -> p c j"), scalar1=1.0, scalar2=0.0, op0=MULT, op1=ADD
+            nc.vector.tensor_copy(
+                out=g2[:].rearrange("p (c i) j -> p c j i", i=4),
+                in_=w2_raw[e][:].rearrange("p j (c i) -> p c j i", i=4),
             )
             live[("g2", e)] = g2
 

@@ -19,8 +19,8 @@ P = 128
 W1_BYTES = 4 * H * 4
 HALF = 512
 LOAD_ORDER = (
-    (1, 0), (2, 0), (1, 1), (2, 1), (0, 0), (1, 2), (2, 2), (1, 3), (2, 3), (1, 4), (2, 4),
-    (1, 5), (1, 6), (1, 7), (0, 1), (2, 5), (2, 6), (2, 7),
+    (1, 0), (1, 1), (2, 0), (1, 2), (2, 1), (0, 0), (1, 3), (2, 2), (1, 4), (2, 3), (1, 5), (2, 4), (0, 1),
+    (1, 6), (2, 5), (1, 7), (2, 6), (2, 7),
 )
 V_TOK = (320, 0)
 
@@ -203,28 +203,23 @@ def tile_routed_moe_kernel(tc, xT, w1, w2, gate, offs, out):
                 op=MULT,
             )
 
-        copy_w2(0)
         gather(1, 0)
         quantise_x(0)
         for p in range(-2, E):
-            if 1 <= p + 3 < E:
-                copy_w2(p + 3)
             if p + 2 < E:
                 copy_w1(p + 2)
             if 0 <= p + 1 < E:
+                copy_w2(p + 1)
                 silu(p + 1)
             if 0 <= p:
                 empty_y(p)
             if p + 2 < E:
                 quantise_w1(p + 2)
                 layer1(p + 2)
-            if p == -2:
-                quantise_w2(0)
             if 0 <= p + 1 < E:
+                quantise_w2(p + 1)
                 quantise_h(p + 1)
                 layer2(p + 1)
-            if 1 <= p + 3 < E:
-                quantise_w2(p + 3)
             if p == -2:
                 gather(1, 1)
                 quantise_x(1)

@@ -17,6 +17,8 @@ ADD = mybir.AluOpType.add
 
 P = 128
 W1_BYTES = 4 * H * 4
+G1_BYTES = 4 * H * 2
+RING = 3
 HALF = 512
 LOAD_ORDER = (
     (1, 0), (1, 1), (2, 0), (1, 2), (2, 1), (0, 0), (1, 3), (2, 2), (1, 4), (2, 3), (1, 5), (2, 4), (0, 1),
@@ -32,6 +34,7 @@ def tile_routed_moe_kernel(tc, xT, w1, w2, gate, offs, out):
         stage = ctx.enter_context(tc.tile_pool(name="stage", bufs=3))
         single = ctx.enter_context(tc.tile_pool(name="single", bufs=2))
         raw1 = ctx.enter_context(tc.tile_pool(name="raw1", bufs=1))
+        ring = ctx.enter_context(tc.tile_pool(name="ring", bufs=1))
         hbank = ctx.enter_context(tc.psum_pool(name="hbank", bufs=3))
         ybank = ctx.enter_context(tc.psum_pool(name="ybank", bufs=3))
 
@@ -111,7 +114,7 @@ def tile_routed_moe_kernel(tc, xT, w1, w2, gate, offs, out):
         live = {}
 
         def copy_w1(e):
-            g1 = stage.tile([P, 4 * H], BF16, name="g1", align_bytes=64)
+            g1 = ring.tile([P, 4 * H], BF16, name="g1_%d" % e, offset=(e % RING) * G1_BYTES, align_bytes=64)
             nc.scalar.copy(
                 out=g1[:].rearrange("p (t m j) -> p m j t", t=4, j=4),
                 in_=w1_raw[e][:].rearrange("p j (m t) -> p m j t", t=4),
@@ -127,15 +130,17 @@ def tile_routed_moe_kernel(tc, xT, w1, w2, gate, offs, out):
 
         def copy_w2(e):
             g2 = single.tile([P, N, 4], BF16, name="g2", align_bytes=64)
-            nc.vector.tensor_copy(
-                out=g2[:].rearrange("p (c i) j -> p c j i", i=4),
-                in_=w2_raw[e][:].rearrange("p j (c i) -> p c j i", i=4),
-            )
+            dst = g2[:].rearrange("p (c i) j -> p c j i", i=4)
+            src = w2_raw[e][:].rearrange("p j (c i) -> p c j i", i=4)
+            if e == E - 1:
+                nc.scalar.copy(out=dst, in_=src)
+            else:
+                nc.vector.tensor_copy(out=dst, in_=src)
             live[("g2", e)] = g2
 
         def quantise_w2(e):
-            c2 = stage.tile([P, N], U32, name="c2", align_bytes=64)
-            s2 = stage.tile([P, N], U8, name="s2", align_bytes=64)
+            c2 = ring.tile([P, N], U32, name="c2_%d" % e, offset=((e + 1) % RING) * G1_BYTES, align_bytes=64)
+            s2 = ring.tile([P, N], U8, name="s2_%d" % e, offset=((e + 1) % RING) * G1_BYTES + 4 * N, align_bytes=64)
             nc.vector.quantize_mx(out=c2[:].bitcast(FP8X4), scales=s2[:], in_=live[("g2", e)][:].rearrange("p c j -> p (c j)"))
             live[("c2", e)] = c2
             live[("s2", e)] = s2

@@ -20,9 +20,10 @@ W1_BYTES = 4 * H * 4
 G1_BYTES = 4 * H * 2
 RING = 3
 HALF = 512
+GATE_SLOTS = 2 * C
 LOAD_ORDER = (
-    (1, 0), (1, 1), (2, 0), (1, 2), (2, 1), (0, 0), (1, 3), (2, 2), (1, 4), (2, 3), (1, 5), (2, 4), (0, 1),
-    (1, 6), (2, 5), (1, 7), (2, 6), (2, 7),
+    (1, 0), (1, 1), (2, 0), (1, 2), (2, 1), (0, 0), (1, 3), (2, 2), (1, 4), (2, 3), (0, 1), (1, 5), (2, 4),
+    (1, 6), (2, 5), (0, 2), (1, 7), (2, 6), (2, 7), (0, 3),
 )
 V_TOK = (320, 0)
 
@@ -56,8 +57,8 @@ def tile_routed_moe_kernel(tc, xT, w1, w2, gate, offs, out):
             w1_raw.append(r1)
             r2 = keep.tile([P, 4, N], F32, name="w2_raw%d" % e)
             w2_raw.append(r2)
-        for v in range(2):
-            gt = keep.tile([P, 2, HALF], F32, name="gate_sb%d" % v)
+        for q in range(E * C // GATE_SLOTS):
+            gt = keep.tile([P, 2, GATE_SLOTS], F32, name="gate_sb%d" % q)
             gate_sb.append(gt)
         for kind, i in LOAD_ORDER:
             if kind == 1:
@@ -65,7 +66,7 @@ def tile_routed_moe_kernel(tc, xT, w1, w2, gate, offs, out):
             elif kind == 2:
                 nc.sync.dma_start(w2_raw[i][:], w2[i].rearrange("(p j) c -> p j c", j=4))
             else:
-                nc.sync.dma_start(gate_sb[i][:], gate_view[:, :, i * HALF : (i + 1) * HALF])
+                nc.sync.dma_start(gate_sb[i][:], gate_view[:, :, i * GATE_SLOTS : (i + 1) * GATE_SLOTS])
 
         warm_in = keep.tile([P, 1], F32, name="warm_in")
         warm_out = keep.tile([P, 1], F32, name="warm_out")
@@ -199,8 +200,8 @@ def tile_routed_moe_kernel(tc, xT, w1, w2, gate, offs, out):
             live[("ys", e)] = ys
 
         def scatter(e, b):
-            g = e * C // HALF
-            s0 = e * C - g * HALF
+            g = e * C // GATE_SLOTS
+            s0 = e * C - g * GATE_SLOTS
             nc.vector.tensor_tensor(
                 out=win[b][:].indirect(offs_sb[:, e * (C // 16) : (e + 1) * (C // 16)]),
                 in0=live[("ys", e)][:, b, :],

@@ -88,14 +88,21 @@ def tile_routed_moe_kernel(tc, xT, w1, w2, gate, offs, out):
         for g in range(2):
             xg = keep.tile([P, HALF, 4], BF16, name="x_grp%d" % g, align_bytes=64)
             x_grp.append(xg)
+        x_words = []
+        for g in range(2):
+            xw = keep.tile([P, 2, HALF], U32, name="x_words%d" % g)
+            x_words.append(xw)
         x_codes = []
         x_scales = []
 
         def gather(u, g):
             window = x_pair[u][:].rearrange("p n e -> p (n e)").bitcast(U32)
-            words = x_grp[g][:].rearrange("p s j -> p (s j)").bitcast(U32).rearrange("p (s u) -> p s u", u=2)
             cols = HALF // 16
-            nc.vector.tensor_copy(out=words[:, :, u], in_=window.indirect(offs_sb[:, g * cols : (g + 1) * cols]))
+            nc.vector.tensor_copy(out=x_words[g][:, u, :], in_=window.indirect(offs_sb[:, g * cols : (g + 1) * cols]))
+
+        def merge(g):
+            words = x_grp[g][:].rearrange("p s j -> p (s j)").bitcast(U32).rearrange("p (s u) -> p s u", u=2)
+            nc.vector.tensor_copy(out=words, in_=x_words[g][:].rearrange("p u s -> p s u"))
 
         def quantise_x(g):
             xc = keep.tile([P, HALF], U32, name="x_codes%d" % g, align_bytes=64)
@@ -210,7 +217,10 @@ def tile_routed_moe_kernel(tc, xT, w1, w2, gate, offs, out):
             )
 
         gather(1, 0)
+        merge(0)
+        gather(1, 1)
         quantise_x(0)
+        merge(1)
         for p in range(-2, E):
             if p + 2 < E:
                 copy_w1(p + 2)
@@ -227,7 +237,6 @@ def tile_routed_moe_kernel(tc, xT, w1, w2, gate, offs, out):
                 quantise_h(p + 1)
                 layer2(p + 1)
             if p == -2:
-                gather(1, 1)
                 quantise_x(1)
             if 0 <= p:
                 scatter(p, 0)

@@ -86,8 +86,9 @@ def tile_routed_moe_kernel(tc, xT, w1, w2, gate, offs, out):
                 nc.scalar.copy(out=dst[:, cut:], in_=src[:, cut:])
         x_grp = []
         for g in range(2):
-            xg = keep.tile([P, HALF, 4], BF16, name="x_grp%d" % g, align_bytes=64)
-            x_grp.append(xg)
+            if g == 0:
+                xg = keep.tile([P, HALF, 4], BF16, name="x_grp0", align_bytes=64)
+                x_grp.append(xg)
         x_words = []
         for g in range(2):
             xw = keep.tile([P, 2, HALF], U32, name="x_words%d" % g)
@@ -220,7 +221,6 @@ def tile_routed_moe_kernel(tc, xT, w1, w2, gate, offs, out):
         merge(0)
         gather(1, 1)
         quantise_x(0)
-        merge(1)
         for p in range(-2, E):
             if p + 2 < E:
                 copy_w1(p + 2)
@@ -237,6 +237,9 @@ def tile_routed_moe_kernel(tc, xT, w1, w2, gate, offs, out):
                 quantise_h(p + 1)
                 layer2(p + 1)
             if p == -2:
+                xg = ring.tile([P, HALF, 4], BF16, name="x_grp1", offset=0, align_bytes=64)
+                x_grp.append(xg)
+                merge(1)
                 quantise_x(1)
             if 0 <= p:
                 scatter(p, 0)

@@ -18,12 +18,13 @@ ADD = mybir.AluOpType.add
 P = 128
 W1_BYTES = 4 * H * 4
 G1_BYTES = 4 * H * 2
+H_BYTES = C * 4 * 2
 RING = 3
 HALF = 512
 GATE_SLOTS = 2 * C
 LOAD_ORDER = (
-    (1, 0), (1, 1), (2, 0), (1, 2), (2, 1), (0, 0), (1, 3), (2, 2), (1, 4), (2, 3), (0, 1), (1, 5), (2, 4),
-    (1, 6), (2, 5), (0, 2), (1, 7), (2, 6), (2, 7), (0, 3),
+    (1, 0), (1, 1), (2, 0), (1, 2), (2, 1), (1, 3), (0, 0), (2, 2), (1, 4), (2, 3), (1, 5), (0, 1), (2, 4),
+    (1, 6), (2, 5), (1, 7), (0, 2), (2, 6), (2, 7), (0, 3),
 )
 V_TOK = (320, 0)
 
@@ -35,6 +36,7 @@ def tile_routed_moe_kernel(tc, xT, w1, w2, gate, offs, out):
         stage = ctx.enter_context(tc.tile_pool(name="stage", bufs=3))
         single = ctx.enter_context(tc.tile_pool(name="single", bufs=2))
         raw1 = ctx.enter_context(tc.tile_pool(name="raw1", bufs=1))
+        hpool = ctx.enter_context(tc.tile_pool(name="hpool", bufs=1))
         ring = ctx.enter_context(tc.tile_pool(name="ring", bufs=1))
         hbank = ctx.enter_context(tc.psum_pool(name="hbank", bufs=3))
         ybank = ctx.enter_context(tc.psum_pool(name="ybank", bufs=3))
@@ -63,6 +65,9 @@ def tile_routed_moe_kernel(tc, xT, w1, w2, gate, offs, out):
         for kind, i in LOAD_ORDER:
             if kind == 1:
                 nc.sync.dma_start(w1_raw[i][:], w1[i].rearrange("(p j) c -> p j c", j=4))
+                if 0 < i < E - 1:
+                    mark = hpool.tile([P, 8], F32, name="mark%d" % i, offset=(i - 1) * H_BYTES, align_bytes=64)
+                    nc.sync.dma_start(mark[0:16, :], w1[i, 0:16, 0:8])
             elif kind == 2:
                 nc.sync.dma_start(w2_raw[i][:], w2[i].rearrange("(p j) c -> p j c", j=4))
             else:
@@ -171,9 +176,10 @@ def tile_routed_moe_kernel(tc, xT, w1, w2, gate, offs, out):
             live[("ph", e)] = ph
 
         def silu(e):
-            hg = raw1.tile(
-                [P, C, 4], BF16, name="hg%d" % e, offset=min(e + 1, E - 1) * W1_BYTES + (e + 1) // E * 2048, align_bytes=64
-            )
+            if e == E - 2:
+                hg = raw1.tile([P, C, 4], BF16, name="hg%d" % e, offset=(E - 1) * W1_BYTES, align_bytes=64)
+            else:
+                hg = hpool.tile([P, C, 4], BF16, name="hg%d" % e, offset=e * H_BYTES, align_bytes=64)
             nc.scalar.activation(out=hg[:], in_=live[("ph", e)][:].rearrange("p t s -> p s t"), func=SILU)
             live[("hg", e)] = hg
 

@@ -26,7 +26,7 @@ LOAD_ORDER = (
     (1, 0), (1, 1), (2, 0), (1, 2), (2, 1), (1, 3), (0, 0), (2, 2), (1, 4), (2, 3), (1, 5), (0, 1), (2, 4),
     (1, 6), (2, 5), (1, 7), (0, 2), (2, 6), (2, 7), (0, 3),
 )
-V_TOK = (320, 0)
+V_TOK = (320, 240)
 
 
 def tile_routed_moe_kernel(tc, xT, w1, w2, gate, offs, out):
@@ -45,11 +45,14 @@ def tile_routed_moe_kernel(tc, xT, w1, w2, gate, offs, out):
         nc.sync.dma_start(offs_sb[:], offs)
         x_view = xT.rearrange("(p t) n -> p t n", t=4)
         x_raw = []
-        for u in range(2):
-            for v in range(2):
-                xr = keep.tile([P, 2, HALF], F32, name="x_raw%d%d" % (u, v))
-                nc.sync.dma_start(xr[:], x_view[:, 2 * u : 2 * u + 2, v * HALF : (v + 1) * HALF])
-                x_raw.append(xr)
+        for v in range(2):
+            xr = keep.tile([P, 2, HALF], F32, name="x_raw0%d" % v)
+            nc.sync.dma_start(xr[:], x_view[:, 0:2, v * HALF : (v + 1) * HALF])
+            x_raw.append(xr[:])
+        xr1 = keep.tile([P, 2, T], F32, name="x_raw1")
+        nc.sync.dma_start(xr1[:], x_view[:, 2:4, :])
+        x_raw.append(xr1[:, :, :HALF])
+        x_raw.append(xr1[:, :, HALF:])
         w1_raw = []
         w2_raw = []
         gate_sb = []
@@ -83,7 +86,7 @@ def tile_routed_moe_kernel(tc, xT, w1, w2, gate, offs, out):
             xb = keep.tile([P, T, 2], BF16, name="x_pair%d" % u)
             x_pair.append(xb)
             for v in range(2):
-                src = x_raw[2 * u + v][:].rearrange("p e (c i) -> p c e i", i=4)
+                src = x_raw[2 * u + v].rearrange("p e (c i) -> p c e i", i=4)
                 dst = xb[:, v * HALF : (v + 1) * HALF, :].rearrange("p (c i) e -> p c e i", i=4)
                 cut = V_TOK[u] // 4
                 if cut > 0:

@@ -42,13 +42,14 @@ def tile_routed_moe_kernel(tc, xT, w1, w2, gate, offs, out):
         ybank = ctx.enter_context(tc.psum_pool(name="ybank", bufs=3))
 
         offs_sb = keep.tile([P, E * C // 16], U16, name="offs_sb")
-        nc.sync.dma_start(offs_sb[:], offs)
         x_view = xT.rearrange("(p t) n -> p t n", t=4)
         x_raw = []
         for v in range(2):
             xr = keep.tile([P, 2, HALF], F32, name="x_raw0%d" % v)
             nc.sync.dma_start(xr[:], x_view[:, 0:2, v * HALF : (v + 1) * HALF])
             x_raw.append(xr[:])
+            if v == 0:
+                nc.sync.dma_start(offs_sb[:], offs)
         xr1 = keep.tile([P, 2, T], F32, name="x_raw1")
         nc.sync.dma_start(xr1[:], x_view[:, 2:4, :])
         x_raw.append(xr1[:, :, :HALF])

from contextlib import ExitStack

import concourse.mybir as mybir

K, T, E, C, H, N = 512, 1024, 8, 128, 512, 256
FLOPS = 2 * E * C * (K * H + H * N)

F32 = mybir.dt.float32
BF16 = mybir.dt.bfloat16
U32 = mybir.dt.uint32
U16 = mybir.dt.uint16
U8 = mybir.dt.uint8
FP8X4 = mybir.dt.float8_e4m3fn_x4
SILU = mybir.ActivationFunctionType.Silu
MULT = mybir.AluOpType.mult
ADD = mybir.AluOpType.add

P = 128
W1_BYTES = 4 * H * 4
G1_BYTES = 4 * H * 2
H_BYTES = C * 4 * 2
RING = 3
HALF = 512
GATE_SLOTS = 2 * C
LOAD_ORDER = (
    (1, 0), (1, 1), (2, 0), (1, 2), (2, 1), (1, 3), (0, 0), (2, 2), (1, 4), (2, 3), (1, 5), (0, 1), (2, 4),
    (1, 6), (2, 5), (1, 7), (0, 2), (2, 6), (2, 7), (0, 3),
)
V_TOK = (320, 240)


def tile_routed_moe_kernel(tc, xT, w1, w2, gate, offs, out):
    nc = tc.nc
    with ExitStack() as ctx:
        keep = ctx.enter_context(tc.tile_pool(name="keep", bufs=1))
        stage = ctx.enter_context(tc.tile_pool(name="stage", bufs=3))
        single = ctx.enter_context(tc.tile_pool(name="single", bufs=2))
        raw1 = ctx.enter_context(tc.tile_pool(name="raw1", bufs=1))
        hpool = ctx.enter_context(tc.tile_pool(name="hpool", bufs=1))
        ring = ctx.enter_context(tc.tile_pool(name="ring", bufs=1))
        hbank = ctx.enter_context(tc.psum_pool(name="hbank", bufs=3))
        ybank = ctx.enter_context(tc.psum_pool(name="ybank", bufs=3))

        offs_sb = keep.tile([P, E * C // 16], U16, name="offs_sb")
        x_view = xT.rearrange("(p t) n -> p t n", t=4)
        x_raw = []
        for v in range(2):
            xr = keep.tile([P, 2, HALF], F32, name="x_raw0%d" % v)
            nc.sync.dma_start(xr[:], x_view[:, 0:2, v * HALF : (v + 1) * HALF])
            x_raw.append(xr[:])
            if v == 0:
                nc.sync.dma_start(offs_sb[:], offs)
        xr1 = keep.tile([P, 2, T], F32, name="x_raw1")
        nc.sync.dma_start(xr1[:], x_view[:, 2:4, :])
        x_raw.append(xr1[:, :, :HALF])
        x_raw.append(xr1[:, :, HALF:])
        w1_raw = []
        w2_raw = []
        gate_sb = []
        gate_view = gate.rearrange("(b p) s -> p b s", p=P)
        for e in range(E):
            r1 = raw1.tile([P, 4, H], F32, name="w1_raw%d" % e, offset=e * W1_BYTES, align_bytes=64)
            w1_raw.append(r1)
            r2 = keep.tile([P, 4, N], F32, name="w2_raw%d" % e)
            w2_raw.append(r2)
        for q in range(E * C // GATE_SLOTS):
            gt = keep.tile([P, 2, GATE_SLOTS], F32, name="gate_sb%d" % q)
            gate_sb.append(gt)
        for kind, i in LOAD_ORDER:
            if kind == 1:
                nc.sync.dma_start(w1_raw[i][:], w1[i].rearrange("(p j) c -> p j c", j=4))
                if 0 < i < E - 1:
                    mark = hpool.tile([P, 8], F32, name="mark%d" % i, offset=(i - 1) * H_BYTES, align_bytes=64)
                    nc.sync.dma_start(mark[0:16, :], w1[i, 0:16, 0:8])
            elif kind == 2:
                nc.sync.dma_start(w2_raw[i][:], w2[i].rearrange("(p j) c -> p j c", j=4))
            else:
                nc.sync.dma_start(gate_sb[i][:], gate_view[:, :, i * GATE_SLOTS : (i + 1) * GATE_SLOTS])

        warm_in = keep.tile([P, 1], F32, name="warm_in")
        warm_out = keep.tile([P, 1], F32, name="warm_out")
        nc.vector.memset(warm_in[:], 0.0)
        nc.scalar.activation(out=warm_out[:], in_=warm_in[:], func=SILU)

        x_pair = []
        for u in range(2):
            xb = keep.tile([P, T, 2], BF16, name="x_pair%d" % u)
            x_pair.append(xb)
            for v in range(2):
                src = x_raw[2 * u + v].rearrange("p e (c i) -> p c e i", i=4)
                dst = xb[:, v * HALF : (v + 1) * HALF, :].rearrange("p (c i) e -> p c e i", i=4)
                cut = V_TOK[u] // 4
                if cut > 0:
                    nc.vector.tensor_copy(out=dst[:, :cut], in_=src[:, :cut])
                nc.scalar.copy(out=dst[:, cut:], in_=src[:, cut:])
        x_grp = []
        for g in range(2):
            if g == 0:
                xg = keep.tile([P, HALF, 4], BF16, name="x_grp0", align_bytes=64)
                x_grp.append(xg)
        x_words = []
        for g in range(2):
            xw = keep.tile([P, 2, HALF], U32, name="x_words%d" % g)
            x_words.append(xw)
        x_codes = []
        x_scales = []

        def gather(u, g):
            window = x_pair[u][:].rearrange("p n e -> p (n e)").bitcast(U32)
            cols = HALF // 16
            nc.vector.tensor_copy(out=x_words[g][:, u, :], in_=window.indirect(offs_sb[:, g * cols : (g + 1) * cols]))

        def merge(g):
            words = x_grp[g][:].rearrange("p s j -> p (s j)").bitcast(U32).rearrange("p (s u) -> p s u", u=2)
            nc.vector.tensor_copy(out=words, in_=x_words[g][:].rearrange("p u s -> p s u"))

        def quantise_x(g):
            xc = keep.tile([P, HALF], U32, name="x_codes%d" % g, align_bytes=64)
            xs = keep.tile([P, HALF], U8, name="x_scales%d" % g, align_bytes=64)
            nc.vector.quantize_mx(out=xc[:].bitcast(FP8X4), scales=xs[:], in_=x_grp[g][:].rearrange("p s j -> p (s j)"))
            x_codes.append(xc)
            x_scales.append(xs)

        gather(0, 0)
        gather(0, 1)

        win = []
        for b in range(2):
            wt = keep.tile([P, T], F32, name="win%d" % b)
            win.append(wt)

        live = {}

        def copy_w1(e):
            g1 = ring.tile([P, 4 * H], BF16, name="g1_%d" % e, offset=(e % RING) * G1_BYTES, align_bytes=64)
            nc.scalar.copy(
                out=g1[:].rearrange("p (t m j) -> p m j t", t=4, j=4),
                in_=w1_raw[e][:].rearrange("p j (m t) -> p m j t", t=4),
            )
            live[("g1", e)] = g1

        def quantise_w1(e):
            c1 = stage.tile([P, H], U32, name="c1", align_bytes=64)
            s1 = stage.tile([P, H], U8, name="s1", align_bytes=64)
            nc.vector.quantize_mx(out=c1[:].bitcast(FP8X4), scales=s1[:], in_=live[("g1", e)][:])
            live[("c1", e)] = c1
            live[("s1", e)] = s1

        def copy_w2(e):
            g2 = single.tile([P, N, 4], BF16, name="g2", align_bytes=64)
            dst = g2[:].rearrange("p (c i) j -> p c j i", i=4)
            src = w2_raw[e][:].rearrange("p j (c i) -> p c j i", i=4)
            if e == E - 1:
                nc.scalar.copy(out=dst, in_=src)
            else:
                nc.vector.tensor_copy(out=dst, in_=src)
            live[("g2", e)] = g2

        def quantise_w2(e):
            c2 = ring.tile([P, N], U32, name="c2_%d" % e, offset=((e + 1) % RING) * G1_BYTES, align_bytes=64)
            s2 = ring.tile([P, N], U8, name="s2_%d" % e, offset=((e + 1) % RING) * G1_BYTES + 4 * N, align_bytes=64)
            nc.vector.quantize_mx(out=c2[:].bitcast(FP8X4), scales=s2[:], in_=live[("g2", e)][:].rearrange("p c j -> p (c j)"))
            live[("c2", e)] = c2
            live[("s2", e)] = s2

        def layer1(e):
            g = e * C // HALF
            s0 = e * C - g * HALF
            ph = hbank.tile([P, 4, C], F32, name="ph")
            for t in range(4):
                nc.tensor.matmul_mx(
                    out=ph[:, t, :],
                    lhsT=live[("c1", e)][:, t * P : (t + 1) * P].bitcast(FP8X4),
                    lhsT_scale=live[("s1", e)][:, t * P : (t + 1) * P],
                    rhs=x_codes[g][:, s0 : s0 + C].bitcast(FP8X4),
                    rhs_scale=x_scales[g][:, s0 : s0 + C],
                    start=True,
                    stop=True,
                )
            live[("ph", e)] = ph

        def silu(e):
            if e == E - 2:
                hg = raw1.tile([P, C, 4], BF16, name="hg%d" % e, offset=(E - 1) * W1_BYTES, align_bytes=64)
            else:
                hg = hpool.tile([P, C, 4], BF16, name="hg%d" % e, offset=e * H_BYTES, align_bytes=64)
            nc.scalar.activation(out=hg[:], in_=live[("ph", e)][:].rearrange("p t s -> p s t"), func=SILU)
            live[("hg", e)] = hg

        def quantise_h(e):
            hc = stage.tile([P, C], U32, name="hc", align_bytes=64)
            hs = stage.tile([P, C], U8, name="hs", align_bytes=64)
            nc.vector.quantize_mx(out=hc[:].bitcast(FP8X4), scales=hs[:], in_=live[("hg", e)][:].rearrange("p s t -> p (s t)"))
            live[("hc", e)] = hc
            live[("hs", e)] = hs

        def layer2(e):
            py = ybank.tile([P, 2, C], F32, name="py")
            for b in range(2):
                nc.tensor.matmul_mx(
                    out=py[:, b, :],
                    lhsT=live[("c2", e)][:, b * P : (b + 1) * P].bitcast(FP8X4),
                    lhsT_scale=live[("s2", e)][:, b * P : (b + 1) * P],
                    rhs=live[("hc", e)][:].bitcast(FP8X4),
                    rhs_scale=live[("hs", e)][:],
                    start=True,
                    stop=True,
                )
            live[("py", e)] = py

        def empty_y(e):
            g = e * C // HALF
            s0 = e * C - g * HALF
            ys = raw1.tile(
                [P, 2, C], F32, name="ys%d" % e, offset=min(e + 2, E - 1) * W1_BYTES + 1024 + max(e + 3 - E, 0) * 2048, align_bytes=64
            )
            nc.scalar.copy(out=ys[:], in_=live[("py", e)][:])
            live[("ys", e)] = ys

        def scatter(e, b):
            g = e * C // GATE_SLOTS
            s0 = e * C - g * GATE_SLOTS
            nc.vector.tensor_tensor(
                out=win[b][:].indirect(offs_sb[:, e * (C // 16) : (e + 1) * (C // 16)]),
                in0=live[("ys", e)][:, b, :],
                in1=gate_sb[g][:, b, s0 : s0 + C],
                op=MULT,
            )

        gather(1, 0)
        merge(0)
        gather(1, 1)
        quantise_x(0)
        for p in range(-2, E):
            if p + 2 < E:
                copy_w1(p + 2)
            if 0 <= p + 1 < E:
                copy_w2(p + 1)
                silu(p + 1)
            if 0 <= p:
                empty_y(p)
            if p + 2 < E:
                quantise_w1(p + 2)
                layer1(p + 2)
            if 0 <= p + 1 < E:
                quantise_w2(p + 1)
                quantise_h(p + 1)
                layer2(p + 1)
            if p == -2:
                xg = ring.tile([P, HALF, 4], BF16, name="x_grp1", offset=0, align_bytes=64)
                x_grp.append(xg)
                merge(1)
                quantise_x(1)
            if 0 <= p:
                scatter(p, 0)
                scatter(p, 1)

        for b in range(2):
            nc.sync.dma_start(out[b * P : (b + 1) * P, :], win[b][:])
